import numpy as np
import ml_dtypes


def mxq(x, axis, fmt="e4m3"):
    dtype, down = {"e4m3": (ml_dtypes.float8_e4m3fn, 7), "e5m2": (ml_dtypes.float8_e5m2, 14)}[fmt]
    v = np.moveaxis(np.asarray(x, np.float32).astype(ml_dtypes.bfloat16).astype(np.float64), axis, -1)
    blocks = v.reshape(v.shape[:-1] + (-1, 32))
    amax = np.abs(blocks).max(-1, keepdims=True)
    byte = np.maximum(np.where(amax > 0, np.frexp(amax)[1] - 1 + 127, 0) - down, 1)
    scale = np.exp2(byte - 127.0)
    codes = (blocks / scale).astype(np.float32).astype(dtype).astype(np.float64)
    return np.moveaxis((codes * scale).reshape(v.shape), -1, axis)


WIDE = False


def mx_kscale(k):
    if not WIDE:
        return np.ones(k)
    levels = np.array([10, -10, 5, -5, 0])
    if k % 512:
        return np.exp2(np.random.permutation(np.resize(levels, k // 32))).repeat(32)
    a = np.empty((k // 512, 16))
    for p in range(k // 512):
        a[p, :8] = np.random.permutation(np.resize(levels, 8))
        for g in range(8):
            far = levels[np.abs(levels - a[p, g]) >= 10]
            a[p, g + 8] = far[np.random.randint(len(far))]
    return np.exp2(a.ravel()).repeat(32)


def f64(x):
    return np.asarray(x).astype(np.float64)


def striped(idx):
    return np.tile(idx.reshape(-1, 16).T, (8, 1)).astype(np.uint16)


def unstriped(offs):
    return offs[:16].T.reshape(-1).astype(np.int64)


K, T, E, C, N = 512, 512, 2, 256, 256


def by_expert(wq, xq):
    return np.concatenate([wq[e].T @ xq[:, e * C:(e + 1) * C] for e in range(E)], axis=1)


def setup_inputs():
    n = np.random.standard_normal
    s = mx_kscale(K)[:, None]
    return {
        "xT": (n((K, T)) * s).astype(np.float32),
        "w": (n((E, K, N)) / np.sqrt(K) / s[None]).astype(np.float32),
        "gate": np.tile(np.random.uniform(0.2, 1.0, E * C), (N, 1)).astype(np.float32),
        "offs": striped(np.random.permutation(T)[:E * C]),
    }


def reference(xT, w, gate, offs):
    idx = unstriped(offs)
    xq = mxq(f64(xT)[:, idx], 0, "e4m3")
    y = by_expert(mxq(f64(w), 1, "e4m3"), xq)
    out = np.zeros((N, T))
    out[:, idx] = f64(gate) * y
    return out

@@ -1,0 +1,128 @@
+from contextlib import ExitStack
+
+import concourse.mybir as mybir
+
+K, T, E, C, N = 512, 512, 2, 256, 256
+FLOPS = 2 * K * N * E * C
+
+F32 = mybir.dt.float32
+BF16 = mybir.dt.bfloat16
+U32 = mybir.dt.uint32
+U16 = mybir.dt.uint16
+U8 = mybir.dt.uint8
+FP8X4 = mybir.dt.float8_e4m3fn_x4
+MULT = mybir.AluOpType.mult
+COPY = mybir.ActivationFunctionType.Copy
+
+P = 128
+PACK = 4
+FB = N // P
+LC = C // 16
+RUN = 8
+
+
+def tile_routed_moe_kernel(tc, xT, w, gate, offs, out):
+    nc = tc.nc
+    with ExitStack() as ctx:
+        keep = ctx.enter_context(tc.tile_pool(name="keep", bufs=1))
+        psum = ctx.enter_context(tc.psum_pool(name="psum", bufs=1))
+
+        one = keep.tile([P, 1], F32, name="one")
+        one_copy = keep.tile([P, 1], F32, name="one_copy")
+        nc.gpsimd.memset(one[:], 0.0)
+        nc.scalar.activation(one_copy[:], one[:], COPY)
+
+        offsets = keep.tile([P, E * C // 16], U16, name="offsets")
+        nc.sync.dma_start(offsets[:], offs)
+
+        x_view = xT.rearrange("(p t) n -> p t n", t=PACK)
+        planes = []
+        for t in range(PACK):
+            plane = keep.tile([P, T], F32, name="plane%d" % t)
+            nc.sync.dma_start(plane[:], x_view[:, t, :])
+            planes.append(plane)
+
+        w_raw = []
+        for e in range(E):
+            raw = keep.tile([P, PACK, N], F32, name="w_raw%d" % e)
+            w_view = w[e].rearrange("(p j) n -> p j n", j=PACK)
+            if e == 0:
+                nc.sync.dma_start(raw[:, :, 0:P], w_view[:, :, 0:P])
+                nc.sync.dma_start(raw[:, :, P:N], w_view[:, :, P:N])
+            else:
+                nc.sync.dma_start(raw[:], w_view)
+            w_raw.append(raw)
+
+        gates = []
+        for f in range(FB):
+            g = keep.tile([P, E * C], F32, name="gate%d" % f)
+            nc.sync.dma_start(g[:], gate[f * P:(f + 1) * P, :])
+            gates.append(g)
+
+        x_bf = keep.tile([P, PACK, T], BF16, name="x_bf")
+        picked = keep.tile([P, PACK, C], F32, name="picked")
+        x_grouped = [keep.tile([P, C, PACK], BF16, name="x_grouped%d" % e, align_bytes=64) for e in range(E)]
+        x_codes = [keep.tile([P, C], U32, name="x_codes%d" % e, align_bytes=64) for e in range(E)]
+        x_scales = [keep.tile([P, C], U8, name="x_scales%d" % e, align_bytes=64) for e in range(E)]
+        w_grouped = [keep.tile([P, N, PACK], BF16, name="w_grouped%d" % e, align_bytes=64) for e in range(E)]
+        w_codes = [keep.tile([P, N], U32, name="w_codes%d" % e, align_bytes=64) for e in range(E)]
+        w_scales = [keep.tile([P, N], U8, name="w_scales%d" % e, align_bytes=64) for e in range(E)]
+        acc = [[psum.tile([P, C], F32, name="acc%d_%d" % (e, f)) for f in range(FB)] for e in range(E)]
+        sums = [[keep.tile([P, C], F32, name="sums%d_%d" % (e, f)) for f in range(FB)] for e in range(E)]
+        windows = [keep.tile([P, T], F32, name="window%d" % f) for f in range(FB)]
+
+        def list_of(e):
+            return offsets[:, e * LC:(e + 1) * LC]
+
+        def group_w(engine_copy, e, lo, hi):
+            engine_copy(out=w_grouped[e][:, lo:hi, :].rearrange("p (c i) j -> p c j i", i=RUN),
+                        in_=w_raw[e][:, :, lo:hi].rearrange("p j (c i) -> p c j i", i=RUN))
+
+        def quant_x(e):
+            nc.vector.quantize_mx(out=x_codes[e][:].bitcast(FP8X4), scales=x_scales[e][:],
+                                  in_=x_grouped[e][:].rearrange("p c t -> p (c t)"))
+
+        def quant_w(e, lo, hi):
+            nc.vector.quantize_mx(out=w_codes[e][:, lo:hi].bitcast(FP8X4), scales=w_scales[e][:, lo:hi],
+                                  in_=w_grouped[e][:, lo:hi, :].rearrange("p n j -> p (n j)"))
+
+        def multiply(e, f):
+            cols = slice(f * P, (f + 1) * P)
+            nc.tensor.matmul_mx(out=acc[e][f][:], lhsT=w_codes[e][:, cols].bitcast(FP8X4),
+                                lhsT_scale=w_scales[e][:, cols], rhs=x_codes[e][:].bitcast(FP8X4),
+                                rhs_scale=x_scales[e][:], start=True, stop=True)
+
+        def scatter(e, f):
+            nc.vector.tensor_tensor(windows[f][:].indirect(list_of(e)),
+                                    sums[e][f][:], gates[f][:, e * C:(e + 1) * C], MULT)
+
+        for t in range(PACK):
+            nc.gpsimd.tensor_copy(out=x_bf[:, t, :], in_=planes[t][:])
+        for t in range(PACK):
+            nc.vector.tensor_copy(picked[:, t, :], planes[t][:].indirect(list_of(0)))
+        for t in range(PACK):
+            nc.scalar.activation(x_grouped[1][:, :, t], x_bf[:, t, :].indirect(list_of(1)), COPY)
+        group_w(nc.vector.tensor_copy, 0, 0, P)
+        nc.vector.tensor_copy(out=x_grouped[0][:].rearrange("p (c i) t -> p c t i", i=RUN),
+                              in_=picked[:].rearrange("p t (c i) -> p c t i", i=RUN))
+        quant_w(0, 0, P)
+        quant_x(0)
+        multiply(0, 0)
+        group_w(nc.vector.tensor_copy, 0, P, N)
+        group_w(nc.vector.tensor_copy, 1, 0, N)
+        quant_w(0, P, N)
+        multiply(0, 1)
+        quant_w(1, 0, N)
+        nc.scalar.copy(out=sums[0][0][:], in_=acc[0][0][:])
+        nc.scalar.copy(out=sums[0][1][:], in_=acc[0][1][:])
+        quant_x(1)
+        multiply(1, 0)
+        multiply(1, 1)
+        scatter(0, 0)
+        nc.scalar.copy(out=sums[1][0][:], in_=acc[1][0][:])
+        nc.scalar.copy(out=sums[1][1][:], in_=acc[1][1][:])
+        scatter(0, 1)
+        scatter(1, 0)
+        nc.sync.dma_start(out[0:P, :], windows[0][:])
+        scatter(1, 1)
+        nc.sync.dma_start(out[P:2 * P, :], windows[1][:])

@@ -33,96 +33,97 @@ def tile_routed_moe_kernel(tc, xT, w, gate, offs, out):
         nc.scalar.activation(one_copy[:], one[:], COPY)
 
         offsets = keep.tile([P, E * C // 16], U16, name="offsets")
-        nc.sync.dma_start(offsets[:], offs)
-
         x_view = xT.rearrange("(p t) n -> p t n", t=PACK)
-        planes = []
-        for t in range(PACK):
-            plane = keep.tile([P, T], F32, name="plane%d" % t)
-            nc.sync.dma_start(plane[:], x_view[:, t, :])
-            planes.append(plane)
-
-        w_raw = []
-        for e in range(E):
-            raw = keep.tile([P, PACK, N], F32, name="w_raw%d" % e)
-            w_view = w[e].rearrange("(p j) n -> p j n", j=PACK)
-            if e == 0:
-                nc.sync.dma_start(raw[:, :, 0:P], w_view[:, :, 0:P])
-                nc.sync.dma_start(raw[:, :, P:N], w_view[:, :, P:N])
-            else:
-                nc.sync.dma_start(raw[:], w_view)
-            w_raw.append(raw)
-
-        gates = []
-        for f in range(FB):
-            g = keep.tile([P, E * C], F32, name="gate%d" % f)
-            nc.sync.dma_start(g[:], gate[f * P:(f + 1) * P, :])
-            gates.append(g)
-
+        w_view = [w[e].rearrange("(p j) n -> p j n", j=PACK) for e in range(E)]
+        nc.sync.dma_start(offsets[:], offs)
+        plane0 = keep.tile([P, T], F32, name="plane0")
+        nc.sync.dma_start(plane0[:], x_view[:, 0, :])
+        plane1 = keep.tile([P, T], F32, name="plane1")
+        nc.sync.dma_start(plane1[:], x_view[:, 1, :])
+        plane2 = keep.tile([P, T], F32, name="plane2")
+        nc.sync.dma_start(plane2[:], x_view[:, 2, :])
+        plane3 = keep.tile([P, T], F32, name="plane3")
+        nc.sync.dma_start(plane3[:], x_view[:, 3, :])
+        w_raw00 = keep.tile([P, PACK, P], F32, name="w_raw00")
+        nc.sync.dma_start(w_raw00[:], w_view[0][:, :, 0:128])
+        w_raw01 = keep.tile([P, PACK, P], F32, name="w_raw01")
+        nc.sync.dma_start(w_raw01[:], w_view[0][:, :, 128:256])
+        w_raw10 = keep.tile([P, PACK, P], F32, name="w_raw10")
+        nc.sync.dma_start(w_raw10[:], w_view[1][:, :, 0:128])
+        w_raw11 = keep.tile([P, PACK, P], F32, name="w_raw11")
+        nc.sync.dma_start(w_raw11[:], w_view[1][:, :, 128:256])
+        gate0 = keep.tile([P, E * C], F32, name="gate0")
+        nc.sync.dma_start(gate0[:], gate[0:128, :])
+        gate1 = keep.tile([P, E * C], F32, name="gate1")
+        nc.sync.dma_start(gate1[:], gate[128:256, :])
         x_bf = keep.tile([P, PACK, T], BF16, name="x_bf")
-        picked = keep.tile([P, PACK, C], F32, name="picked")
-        x_grouped = [keep.tile([P, C, PACK], BF16, name="x_grouped%d" % e, align_bytes=64) for e in range(E)]
-        x_codes = [keep.tile([P, C], U32, name="x_codes%d" % e, align_bytes=64) for e in range(E)]
-        x_scales = [keep.tile([P, C], U8, name="x_scales%d" % e, align_bytes=64) for e in range(E)]
-        w_grouped = [keep.tile([P, N, PACK], BF16, name="w_grouped%d" % e, align_bytes=64) for e in range(E)]
-        w_codes = [keep.tile([P, N], U32, name="w_codes%d" % e, align_bytes=64) for e in range(E)]
-        w_scales = [keep.tile([P, N], U8, name="w_scales%d" % e, align_bytes=64) for e in range(E)]
-        acc = [[psum.tile([P, C], F32, name="acc%d_%d" % (e, f)) for f in range(FB)] for e in range(E)]
-        sums = [[keep.tile([P, C], F32, name="sums%d_%d" % (e, f)) for f in range(FB)] for e in range(E)]
-        windows = [keep.tile([P, T], F32, name="window%d" % f) for f in range(FB)]
-
-        def list_of(e):
-            return offsets[:, e * LC:(e + 1) * LC]
-
-        def group_w(engine_copy, e, lo, hi):
-            engine_copy(out=w_grouped[e][:, lo:hi, :].rearrange("p (c i) j -> p c j i", i=RUN),
-                        in_=w_raw[e][:, :, lo:hi].rearrange("p j (c i) -> p c j i", i=RUN))
-
-        def quant_x(e):
-            nc.vector.quantize_mx(out=x_codes[e][:].bitcast(FP8X4), scales=x_scales[e][:],
-                                  in_=x_grouped[e][:].rearrange("p c t -> p (c t)"))
-
-        def quant_w(e, lo, hi):
-            nc.vector.quantize_mx(out=w_codes[e][:, lo:hi].bitcast(FP8X4), scales=w_scales[e][:, lo:hi],
-                                  in_=w_grouped[e][:, lo:hi, :].rearrange("p n j -> p (n j)"))
-
-        def multiply(e, f):
-            cols = slice(f * P, (f + 1) * P)
-            nc.tensor.matmul_mx(out=acc[e][f][:], lhsT=w_codes[e][:, cols].bitcast(FP8X4),
-                                lhsT_scale=w_scales[e][:, cols], rhs=x_codes[e][:].bitcast(FP8X4),
-                                rhs_scale=x_scales[e][:], start=True, stop=True)
-
-        def scatter(e, f):
-            nc.vector.tensor_tensor(windows[f][:].indirect(list_of(e)),
-                                    sums[e][f][:], gates[f][:, e * C:(e + 1) * C], MULT)
-
-        for t in range(PACK):
-            nc.gpsimd.tensor_copy(out=x_bf[:, t, :], in_=planes[t][:])
-        for t in range(PACK):
-            nc.vector.tensor_copy(picked[:, t, :], planes[t][:].indirect(list_of(0)))
-        for t in range(PACK):
-            nc.scalar.activation(x_grouped[1][:, :, t], x_bf[:, t, :].indirect(list_of(1)), COPY)
-        group_w(nc.vector.tensor_copy, 0, 0, P)
-        nc.vector.tensor_copy(out=x_grouped[0][:].rearrange("p (c i) t -> p c t i", i=RUN),
-                              in_=picked[:].rearrange("p t (c i) -> p c t i", i=RUN))
-        quant_w(0, 0, P)
-        quant_x(0)
-        multiply(0, 0)
-        group_w(nc.vector.tensor_copy, 0, P, N)
-        group_w(nc.vector.tensor_copy, 1, 0, N)
-        quant_w(0, P, N)
-        multiply(0, 1)
-        quant_w(1, 0, N)
-        nc.scalar.copy(out=sums[0][0][:], in_=acc[0][0][:])
-        nc.scalar.copy(out=sums[0][1][:], in_=acc[0][1][:])
-        quant_x(1)
-        multiply(1, 0)
-        multiply(1, 1)
-        scatter(0, 0)
-        nc.scalar.copy(out=sums[1][0][:], in_=acc[1][0][:])
-        nc.scalar.copy(out=sums[1][1][:], in_=acc[1][1][:])
-        scatter(0, 1)
-        scatter(1, 0)
-        nc.sync.dma_start(out[0:P, :], windows[0][:])
-        scatter(1, 1)
-        nc.sync.dma_start(out[P:2 * P, :], windows[1][:])
+        nc.gpsimd.tensor_copy(out=x_bf[:, 0, :], in_=plane0[:])
+        nc.gpsimd.tensor_copy(out=x_bf[:, 1, :], in_=plane1[:])
+        nc.gpsimd.tensor_copy(out=x_bf[:, 2, :], in_=plane2[:])
+        nc.gpsimd.tensor_copy(out=x_bf[:, 3, :], in_=plane3[:])
+        picked = keep.tile([P, PACK, 256], F32, name="picked")
+        nc.vector.tensor_copy(picked[:, 0, :], plane0[:].indirect(offsets[:, 0:16]))
+        nc.vector.tensor_copy(picked[:, 1, :], plane1[:].indirect(offsets[:, 0:16]))
+        nc.vector.tensor_copy(picked[:, 2, :], plane2[:].indirect(offsets[:, 0:16]))
+        nc.vector.tensor_copy(picked[:, 3, :], plane3[:].indirect(offsets[:, 0:16]))
+        x_e = keep.tile([P, 256, PACK], BF16, name="x_e", align_bytes=64)
+        nc.scalar.activation(x_e[:, 0:256, 0], x_bf[:, 0, :].indirect(offsets[:, 16:32]), COPY)
+        nc.scalar.activation(x_e[:, 0:256, 1], x_bf[:, 1, :].indirect(offsets[:, 16:32]), COPY)
+        nc.scalar.activation(x_e[:, 0:256, 2], x_bf[:, 2, :].indirect(offsets[:, 16:32]), COPY)
+        nc.scalar.activation(x_e[:, 0:256, 3], x_bf[:, 3, :].indirect(offsets[:, 16:32]), COPY)
+        w_grouped00 = keep.tile([P, P, PACK], BF16, name="w_grouped00", align_bytes=64)
+        nc.vector.tensor_copy(out=w_grouped00[:].rearrange("p (c i) j -> p c j i", i=RUN), in_=w_raw00[:].rearrange("p j (c i) -> p c j i", i=RUN))
+        x_a = keep.tile([P, 256, PACK], BF16, name="x_a", align_bytes=64)
+        nc.vector.tensor_copy(out=x_a[:].rearrange("p (c i) t -> p c t i", i=RUN), in_=picked[:].rearrange("p t (c i) -> p c t i", i=RUN))
+        w_codes00 = keep.tile([P, P], U32, name="w_codes00", align_bytes=64)
+        w_scales00 = keep.tile([P, P], U8, name="w_scales00", align_bytes=64)
+        nc.vector.quantize_mx(out=w_codes00[:].bitcast(FP8X4), scales=w_scales00[:], in_=w_grouped00[:].rearrange("p n j -> p (n j)"))
+        a_codes = keep.tile([P, 256], U32, name="a_codes", align_bytes=64)
+        a_scales = keep.tile([P, 256], U8, name="a_scales", align_bytes=64)
+        nc.vector.quantize_mx(out=a_codes[:].bitcast(FP8X4), scales=a_scales[:], in_=x_a[:].rearrange("p c t -> p (c t)"))
+        acc_a0 = psum.tile([P, 256], F32, name="acc_a0")
+        nc.tensor.matmul_mx(out=acc_a0[:], lhsT=w_codes00[:].bitcast(FP8X4), lhsT_scale=w_scales00[:],
+                            rhs=a_codes[:].bitcast(FP8X4), rhs_scale=a_scales[:], start=True, stop=True)
+        w_grouped01 = keep.tile([P, P, PACK], BF16, name="w_grouped01", align_bytes=64)
+        nc.vector.tensor_copy(out=w_grouped01[:].rearrange("p (c i) j -> p c j i", i=RUN), in_=w_raw01[:].rearrange("p j (c i) -> p c j i", i=RUN))
+        w_grouped10 = keep.tile([P, P, PACK], BF16, name="w_grouped10", align_bytes=64)
+        nc.vector.tensor_copy(out=w_grouped10[:].rearrange("p (c i) j -> p c j i", i=RUN), in_=w_raw10[:].rearrange("p j (c i) -> p c j i", i=RUN))
+        w_codes01 = keep.tile([P, P], U32, name="w_codes01", align_bytes=64)
+        w_scales01 = keep.tile([P, P], U8, name="w_scales01", align_bytes=64)
+        nc.vector.quantize_mx(out=w_codes01[:].bitcast(FP8X4), scales=w_scales01[:], in_=w_grouped01[:].rearrange("p n j -> p (n j)"))
+        e_codes = keep.tile([P, 256], U32, name="e_codes", align_bytes=64)
+        e_scales = keep.tile([P, 256], U8, name="e_scales", align_bytes=64)
+        nc.vector.quantize_mx(out=e_codes[:].bitcast(FP8X4), scales=e_scales[:], in_=x_e[:, 0:256, :].rearrange("p c t -> p (c t)"))
+        w_codes10 = keep.tile([P, P], U32, name="w_codes10", align_bytes=64)
+        w_scales10 = keep.tile([P, P], U8, name="w_scales10", align_bytes=64)
+        nc.vector.quantize_mx(out=w_codes10[:].bitcast(FP8X4), scales=w_scales10[:], in_=w_grouped10[:].rearrange("p n j -> p (n j)"))
+        w_grouped11 = keep.tile([P, P, PACK], BF16, name="w_grouped11", align_bytes=64)
+        nc.scalar.copy(out=w_grouped11[:].rearrange("p (c i) j -> p c j i", i=RUN), in_=w_raw11[:].rearrange("p j (c i) -> p c j i", i=RUN))
+        w_codes11 = keep.tile([P, P], U32, name="w_codes11", align_bytes=64)
+        w_scales11 = keep.tile([P, P], U8, name="w_scales11", align_bytes=64)
+        nc.vector.quantize_mx(out=w_codes11[:].bitcast(FP8X4), scales=w_scales11[:], in_=w_grouped11[:].rearrange("p n j -> p (n j)"))
+        acc_a1 = psum.tile([P, 256], F32, name="acc_a1")
+        nc.tensor.matmul_mx(out=acc_a1[:], lhsT=w_codes01[:].bitcast(FP8X4), lhsT_scale=w_scales01[:],
+                            rhs=a_codes[:].bitcast(FP8X4), rhs_scale=a_scales[:], start=True, stop=True)
+        sums_a0 = keep.tile([P, 256], F32, name="sums_a0")
+        nc.scalar.copy(out=sums_a0[:], in_=acc_a0[:])
+        acc_e0 = psum.tile([P, 256], F32, name="acc_e0")
+        nc.tensor.matmul_mx(out=acc_e0[:], lhsT=w_codes10[:].bitcast(FP8X4), lhsT_scale=w_scales10[:],
+                            rhs=e_codes[:].bitcast(FP8X4), rhs_scale=e_scales[:], start=True, stop=True)
+        acc_e1 = psum.tile([P, 256], F32, name="acc_e1")
+        nc.tensor.matmul_mx(out=acc_e1[:], lhsT=w_codes11[:].bitcast(FP8X4), lhsT_scale=w_scales11[:],
+                            rhs=e_codes[:].bitcast(FP8X4), rhs_scale=e_scales[:], start=True, stop=True)
+        sums_a1 = keep.tile([P, 256], F32, name="sums_a1")
+        nc.scalar.copy(out=sums_a1[:], in_=acc_a1[:])
+        sums_e0 = keep.tile([P, 256], F32, name="sums_e0")
+        nc.scalar.copy(out=sums_e0[:], in_=acc_e0[:])
+        sums_e1 = keep.tile([P, 256], F32, name="sums_e1")
+        nc.scalar.copy(out=sums_e1[:], in_=acc_e1[:])
+        window0 = keep.tile([P, T], F32, name="window0")
+        nc.vector.tensor_tensor(window0[:].indirect(offsets[:, 0:16]), sums_a0[:], gate0[:, 0:256], MULT)
+        window1 = keep.tile([P, T], F32, name="window1")
+        nc.vector.tensor_tensor(window1[:].indirect(offsets[:, 0:16]), sums_a1[:], gate1[:, 0:256], MULT)
+        nc.vector.tensor_tensor(window0[:].indirect(offsets[:, 16:32]), sums_e0[:], gate0[:, 256:512], MULT)
+        nc.sync.dma_start(out[0:128, :], window0[:])
+        nc.vector.tensor_tensor(window1[:].indirect(offsets[:, 16:32]), sums_e1[:], gate1[:, 256:512], MULT)
+        nc.sync.dma_start(out[128:256, :], window1[:])

@@ -35,9 +35,9 @@ def tile_routed_moe_kernel(tc, xT, w, gate, offs, out):
         offsets = keep.tile([P, E * C // 16], U16, name="offsets")
         x_view = xT.rearrange("(p t) n -> p t n", t=PACK)
         w_view = [w[e].rearrange("(p j) n -> p j n", j=PACK) for e in range(E)]
-        nc.sync.dma_start(offsets[:], offs)
         plane0 = keep.tile([P, T], F32, name="plane0")
         nc.sync.dma_start(plane0[:], x_view[:, 0, :])
+        nc.sync.dma_start(offsets[:], offs)
         plane1 = keep.tile([P, T], F32, name="plane1")
         nc.sync.dma_start(plane1[:], x_view[:, 1, :])
         plane2 = keep.tile([P, T], F32, name="plane2")
@@ -87,7 +87,9 @@ def tile_routed_moe_kernel(tc, xT, w, gate, offs, out):
         w_grouped01 = keep.tile([P, P, PACK], BF16, name="w_grouped01", align_bytes=64)
         nc.vector.tensor_copy(out=w_grouped01[:].rearrange("p (c i) j -> p c j i", i=RUN), in_=w_raw01[:].rearrange("p j (c i) -> p c j i", i=RUN))
         w_grouped10 = keep.tile([P, P, PACK], BF16, name="w_grouped10", align_bytes=64)
-        nc.vector.tensor_copy(out=w_grouped10[:].rearrange("p (c i) j -> p c j i", i=RUN), in_=w_raw10[:].rearrange("p j (c i) -> p c j i", i=RUN))
+        nc.scalar.copy(out=w_grouped10[:].rearrange("p (c i) j -> p c j i", i=RUN), in_=w_raw10[:].rearrange("p j (c i) -> p c j i", i=RUN))
+        w_grouped11 = keep.tile([P, P, PACK], BF16, name="w_grouped11", align_bytes=64)
+        nc.vector.tensor_copy(out=w_grouped11[:].rearrange("p (c i) j -> p c j i", i=RUN), in_=w_raw11[:].rearrange("p j (c i) -> p c j i", i=RUN))
         w_codes01 = keep.tile([P, P], U32, name="w_codes01", align_bytes=64)
         w_scales01 = keep.tile([P, P], U8, name="w_scales01", align_bytes=64)
         nc.vector.quantize_mx(out=w_codes01[:].bitcast(FP8X4), scales=w_scales01[:], in_=w_grouped01[:].rearrange("p n j -> p (n j)"))
@@ -97,8 +99,6 @@ def tile_routed_moe_kernel(tc, xT, w, gate, offs, out):
         w_codes10 = keep.tile([P, P], U32, name="w_codes10", align_bytes=64)
         w_scales10 = keep.tile([P, P], U8, name="w_scales10", align_bytes=64)
         nc.vector.quantize_mx(out=w_codes10[:].bitcast(FP8X4), scales=w_scales10[:], in_=w_grouped10[:].rearrange("p n j -> p (n j)"))
-        w_grouped11 = keep.tile([P, P, PACK], BF16, name="w_grouped11", align_bytes=64)
-        nc.scalar.copy(out=w_grouped11[:].rearrange("p (c i) j -> p c j i", i=RUN), in_=w_raw11[:].rearrange("p j (c i) -> p c j i", i=RUN))
         w_codes11 = keep.tile([P, P], U32, name="w_codes11", align_bytes=64)
         w_scales11 = keep.tile([P, P], U8, name="w_scales11", align_bytes=64)
         nc.vector.quantize_mx(out=w_codes11[:].bitcast(FP8X4), scales=w_scales11[:], in_=w_grouped11[:].rearrange("p n j -> p (n j)"))

@@ -52,10 +52,10 @@ def tile_routed_moe_kernel(tc, xT, w, gate, offs, out):
         nc.sync.dma_start(w_raw10[:], w_view[1][:, :, 0:128])
         w_raw11 = keep.tile([P, PACK, P], F32, name="w_raw11")
         nc.sync.dma_start(w_raw11[:], w_view[1][:, :, 128:256])
-        gate0 = keep.tile([P, E * C], F32, name="gate0")
-        nc.sync.dma_start(gate0[:], gate[0:128, :])
-        gate1 = keep.tile([P, E * C], F32, name="gate1")
-        nc.sync.dma_start(gate1[:], gate[128:256, :])
+        gates = [[keep.tile([P, C], F32, name="gate%d_%d" % (e, f)) for f in range(FB)] for e in range(E)]
+        for e in range(E):
+            for f in range(FB):
+                nc.sync.dma_start(gates[e][f][:], gate[f * P:(f + 1) * P, e * C:(e + 1) * C])
         x_bf = keep.tile([P, PACK, T], BF16, name="x_bf")
         nc.gpsimd.tensor_copy(out=x_bf[:, 0, :], in_=plane0[:])
         nc.gpsimd.tensor_copy(out=x_bf[:, 1, :], in_=plane1[:])
@@ -120,10 +120,10 @@ def tile_routed_moe_kernel(tc, xT, w, gate, offs, out):
         sums_e1 = keep.tile([P, 256], F32, name="sums_e1")
         nc.scalar.copy(out=sums_e1[:], in_=acc_e1[:])
         window0 = keep.tile([P, T], F32, name="window0")
-        nc.vector.tensor_tensor(window0[:].indirect(offsets[:, 0:16]), sums_a0[:], gate0[:, 0:256], MULT)
+        nc.vector.tensor_tensor(window0[:].indirect(offsets[:, 0:16]), sums_a0[:], gates[0][0][:], MULT)
         window1 = keep.tile([P, T], F32, name="window1")
-        nc.vector.tensor_tensor(window1[:].indirect(offsets[:, 0:16]), sums_a1[:], gate1[:, 0:256], MULT)
-        nc.vector.tensor_tensor(window0[:].indirect(offsets[:, 16:32]), sums_e0[:], gate0[:, 256:512], MULT)
+        nc.vector.tensor_tensor(window1[:].indirect(offsets[:, 0:16]), sums_a1[:], gates[0][1][:], MULT)
+        nc.vector.tensor_tensor(window0[:].indirect(offsets[:, 16:32]), sums_e0[:], gates[1][0][:], MULT)
         nc.sync.dma_start(out[0:128, :], window0[:])
-        nc.vector.tensor_tensor(window1[:].indirect(offsets[:, 16:32]), sums_e1[:], gate1[:, 256:512], MULT)
+        nc.vector.tensor_tensor(window1[:].indirect(offsets[:, 16:32]), sums_e1[:], gates[1][1][:], MULT)
         nc.sync.dma_start(out[128:256, :], window1[:])

from contextlib import ExitStack

import concourse.mybir as mybir

K, T, E, C, N = 512, 512, 2, 256, 256
FLOPS = 2 * K * N * E * C

F32 = mybir.dt.float32
BF16 = mybir.dt.bfloat16
U32 = mybir.dt.uint32
U16 = mybir.dt.uint16
U8 = mybir.dt.uint8
FP8X4 = mybir.dt.float8_e4m3fn_x4
MULT = mybir.AluOpType.mult
COPY = mybir.ActivationFunctionType.Copy

P = 128
PACK = 4
FB = N // P
LC = C // 16
RUN = 8


def tile_routed_moe_kernel(tc, xT, w, gate, offs, out):
    nc = tc.nc
    with ExitStack() as ctx:
        keep = ctx.enter_context(tc.tile_pool(name="keep", bufs=1))
        psum = ctx.enter_context(tc.psum_pool(name="psum", bufs=1))

        one = keep.tile([P, 1], F32, name="one")
        one_copy = keep.tile([P, 1], F32, name="one_copy")
        nc.gpsimd.memset(one[:], 0.0)
        nc.scalar.activation(one_copy[:], one[:], COPY)

        offsets = keep.tile([P, E * C // 16], U16, name="offsets")
        x_view = xT.rearrange("(p t) n -> p t n", t=PACK)
        w_view = [w[e].rearrange("(p j) n -> p j n", j=PACK) for e in range(E)]
        plane0 = keep.tile([P, T], F32, name="plane0")
        nc.sync.dma_start(plane0[:], x_view[:, 0, :])
        nc.sync.dma_start(offsets[:], offs)
        plane1 = keep.tile([P, T], F32, name="plane1")
        nc.sync.dma_start(plane1[:], x_view[:, 1, :])
        plane2 = keep.tile([P, T], F32, name="plane2")
        nc.sync.dma_start(plane2[:], x_view[:, 2, :])
        plane3 = keep.tile([P, T], F32, name="plane3")
        nc.sync.dma_start(plane3[:], x_view[:, 3, :])
        w_raw00 = keep.tile([P, PACK, P], F32, name="w_raw00")
        nc.sync.dma_start(w_raw00[:], w_view[0][:, :, 0:128])
        w_raw01 = keep.tile([P, PACK, P], F32, name="w_raw01")
        nc.sync.dma_start(w_raw01[:], w_view[0][:, :, 128:256])
        w_raw10 = keep.tile([P, PACK, P], F32, name="w_raw10")
        nc.sync.dma_start(w_raw10[:], w_view[1][:, :, 0:128])
        w_raw11 = keep.tile([P, PACK, P], F32, name="w_raw11")
        nc.sync.dma_start(w_raw11[:], w_view[1][:, :, 128:256])
        gates = [[keep.tile([P, C], F32, name="gate%d_%d" % (e, f)) for f in range(FB)] for e in range(E)]
        for e in range(E):
            for f in range(FB):
                nc.sync.dma_start(gates[e][f][:], gate[f * P:(f + 1) * P, e * C:(e + 1) * C])
        x_bf = keep.tile([P, PACK, T], BF16, name="x_bf")
        nc.gpsimd.tensor_copy(out=x_bf[:, 0, :], in_=plane0[:])
        nc.gpsimd.tensor_copy(out=x_bf[:, 1, :], in_=plane1[:])
        nc.gpsimd.tensor_copy(out=x_bf[:, 2, :], in_=plane2[:])
        nc.gpsimd.tensor_copy(out=x_bf[:, 3, :], in_=plane3[:])
        picked = keep.tile([P, PACK, 256], F32, name="picked")
        nc.vector.tensor_copy(picked[:, 0, :], plane0[:].indirect(offsets[:, 0:16]))
        nc.vector.tensor_copy(picked[:, 1, :], plane1[:].indirect(offsets[:, 0:16]))
        nc.vector.tensor_copy(picked[:, 2, :], plane2[:].indirect(offsets[:, 0:16]))
        nc.vector.tensor_copy(picked[:, 3, :], plane3[:].indirect(offsets[:, 0:16]))
        x_e = keep.tile([P, 256, PACK], BF16, name="x_e", align_bytes=64)
        nc.scalar.activation(x_e[:, 0:256, 0], x_bf[:, 0, :].indirect(offsets[:, 16:32]), COPY)
        nc.scalar.activation(x_e[:, 0:256, 1], x_bf[:, 1, :].indirect(offsets[:, 16:32]), COPY)
        nc.scalar.activation(x_e[:, 0:256, 2], x_bf[:, 2, :].indirect(offsets[:, 16:32]), COPY)
        nc.scalar.activation(x_e[:, 0:256, 3], x_bf[:, 3, :].indirect(offsets[:, 16:32]), COPY)
        w_grouped00 = keep.tile([P, P, PACK], BF16, name="w_grouped00", align_bytes=64)
        nc.vector.tensor_copy(out=w_grouped00[:].rearrange("p (c i) j -> p c j i", i=RUN), in_=w_raw00[:].rearrange("p j (c i) -> p c j i", i=RUN))
        x_a = keep.tile([P, 256, PACK], BF16, name="x_a", align_bytes=64)
        nc.vector.tensor_copy(out=x_a[:].rearrange("p (c i) t -> p c t i", i=RUN), in_=picked[:].rearrange("p t (c i) -> p c t i", i=RUN))
        w_codes00 = keep.tile([P, P], U32, name="w_codes00", align_bytes=64)
        w_scales00 = keep.tile([P, P], U8, name="w_scales00", align_bytes=64)
        nc.vector.quantize_mx(out=w_codes00[:].bitcast(FP8X4), scales=w_scales00[:], in_=w_grouped00[:].rearrange("p n j -> p (n j)"))
        a_codes = keep.tile([P, 256], U32, name="a_codes", align_bytes=64)
        a_scales = keep.tile([P, 256], U8, name="a_scales", align_bytes=64)
        nc.vector.quantize_mx(out=a_codes[:].bitcast(FP8X4), scales=a_scales[:], in_=x_a[:].rearrange("p c t -> p (c t)"))
        acc_a0 = psum.tile([P, 256], F32, name="acc_a0")
        nc.tensor.matmul_mx(out=acc_a0[:], lhsT=w_codes00[:].bitcast(FP8X4), lhsT_scale=w_scales00[:],
                            rhs=a_codes[:].bitcast(FP8X4), rhs_scale=a_scales[:], start=True, stop=True)
        w_grouped01 = keep.tile([P, P, PACK], BF16, name="w_grouped01", align_bytes=64)
        nc.vector.tensor_copy(out=w_grouped01[:].rearrange("p (c i) j -> p c j i", i=RUN), in_=w_raw01[:].rearrange("p j (c i) -> p c j i", i=RUN))
        w_grouped10 = keep.tile([P, P, PACK], BF16, name="w_grouped10", align_bytes=64)
        nc.scalar.copy(out=w_grouped10[:].rearrange("p (c i) j -> p c j i", i=RUN), in_=w_raw10[:].rearrange("p j (c i) -> p c j i", i=RUN))
        w_grouped11 = keep.tile([P, P, PACK], BF16, name="w_grouped11", align_bytes=64)
        nc.vector.tensor_copy(out=w_grouped11[:].rearrange("p (c i) j -> p c j i", i=RUN), in_=w_raw11[:].rearrange("p j (c i) -> p c j i", i=RUN))
        w_codes01 = keep.tile([P, P], U32, name="w_codes01", align_bytes=64)
        w_scales01 = keep.tile([P, P], U8, name="w_scales01", align_bytes=64)
        nc.vector.quantize_mx(out=w_codes01[:].bitcast(FP8X4), scales=w_scales01[:], in_=w_grouped01[:].rearrange("p n j -> p (n j)"))
        e_codes = keep.tile([P, 256], U32, name="e_codes", align_bytes=64)
        e_scales = keep.tile([P, 256], U8, name="e_scales", align_bytes=64)
        nc.vector.quantize_mx(out=e_codes[:].bitcast(FP8X4), scales=e_scales[:], in_=x_e[:, 0:256, :].rearrange("p c t -> p (c t)"))
        w_codes10 = keep.tile([P, P], U32, name="w_codes10", align_bytes=64)
        w_scales10 = keep.tile([P, P], U8, name="w_scales10", align_bytes=64)
        nc.vector.quantize_mx(out=w_codes10[:].bitcast(FP8X4), scales=w_scales10[:], in_=w_grouped10[:].rearrange("p n j -> p (n j)"))
        w_codes11 = keep.tile([P, P], U32, name="w_codes11", align_bytes=64)
        w_scales11 = keep.tile([P, P], U8, name="w_scales11", align_bytes=64)
        nc.vector.quantize_mx(out=w_codes11[:].bitcast(FP8X4), scales=w_scales11[:], in_=w_grouped11[:].rearrange("p n j -> p (n j)"))
        acc_a1 = psum.tile([P, 256], F32, name="acc_a1")
        nc.tensor.matmul_mx(out=acc_a1[:], lhsT=w_codes01[:].bitcast(FP8X4), lhsT_scale=w_scales01[:],
                            rhs=a_codes[:].bitcast(FP8X4), rhs_scale=a_scales[:], start=True, stop=True)
        sums_a0 = keep.tile([P, 256], F32, name="sums_a0")
        nc.scalar.copy(out=sums_a0[:], in_=acc_a0[:])
        acc_e0 = psum.tile([P, 256], F32, name="acc_e0")
        nc.tensor.matmul_mx(out=acc_e0[:], lhsT=w_codes10[:].bitcast(FP8X4), lhsT_scale=w_scales10[:],
                            rhs=e_codes[:].bitcast(FP8X4), rhs_scale=e_scales[:], start=True, stop=True)
        acc_e1 = psum.tile([P, 256], F32, name="acc_e1")
        nc.tensor.matmul_mx(out=acc_e1[:], lhsT=w_codes11[:].bitcast(FP8X4), lhsT_scale=w_scales11[:],
                            rhs=e_codes[:].bitcast(FP8X4), rhs_scale=e_scales[:], start=True, stop=True)
        sums_a1 = keep.tile([P, 256], F32, name="sums_a1")
        nc.scalar.copy(out=sums_a1[:], in_=acc_a1[:])
        sums_e0 = keep.tile([P, 256], F32, name="sums_e0")
        nc.scalar.copy(out=sums_e0[:], in_=acc_e0[:])
        sums_e1 = keep.tile([P, 256], F32, name="sums_e1")
        nc.scalar.copy(out=sums_e1[:], in_=acc_e1[:])
        window0 = keep.tile([P, T], F32, name="window0")
        nc.vector.tensor_tensor(window0[:].indirect(offsets[:, 0:16]), sums_a0[:], gates[0][0][:], MULT)
        window1 = keep.tile([P, T], F32, name="window1")
        nc.vector.tensor_tensor(window1[:].indirect(offsets[:, 0:16]), sums_a1[:], gates[0][1][:], MULT)
        nc.vector.tensor_tensor(window0[:].indirect(offsets[:, 16:32]), sums_e0[:], gates[1][0][:], MULT)
        nc.sync.dma_start(out[0:128, :], window0[:])
        nc.vector.tensor_tensor(window1[:].indirect(offsets[:, 16:32]), sums_e1[:], gates[1][1][:], MULT)
        nc.sync.dma_start(out[128:256, :], window1[:])
